import numpy as np
import ml_dtypes


def mxq(x, axis, fmt="e4m3"):
    dtype, down = {"e4m3": (ml_dtypes.float8_e4m3fn, 7), "e5m2": (ml_dtypes.float8_e5m2, 14)}[fmt]
    v = np.moveaxis(np.asarray(x, np.float32).astype(ml_dtypes.bfloat16).astype(np.float64), axis, -1)
    blocks = v.reshape(v.shape[:-1] + (-1, 32))
    amax = np.abs(blocks).max(-1, keepdims=True)
    byte = np.maximum(np.where(amax > 0, np.frexp(amax)[1] - 1 + 127, 0) - down, 1)
    scale = np.exp2(byte - 127.0)
    codes = (blocks / scale).astype(np.float32).astype(dtype).astype(np.float64)
    return np.moveaxis((codes * scale).reshape(v.shape), -1, axis)


WIDE = False


def mx_kscale(k):
    if not WIDE:
        return np.ones(k)
    levels = np.array([10, -10, 5, -5, 0])
    if k % 512:
        return np.exp2(np.random.permutation(np.resize(levels, k // 32))).repeat(32)
    a = np.empty((k // 512, 16))
    for p in range(k // 512):
        a[p, :8] = np.random.permutation(np.resize(levels, 8))
        for g in range(8):
            far = levels[np.abs(levels - a[p, g]) >= 10]
            a[p, g + 8] = far[np.random.randint(len(far))]
    return np.exp2(a.ravel()).repeat(32)


def f64(x):
    return np.asarray(x).astype(np.float64)


def striped(idx):
    return np.tile(idx.reshape(-1, 16).T, (8, 1)).astype(np.uint16)


def unstriped(offs):
    return offs[:16].T.reshape(-1).astype(np.int64)


def striped8(idx):
    return np.concatenate([x.reshape(-1, 16).T for x in idx]).astype(np.uint16)


def runs(offs, k):
    lists = np.stack([offs[16 * r : 16 * r + 16].T.reshape(-1) for r in range(8)]).astype(np.int64)
    return lists[np.arange(k) % 512 // 64]


def pack_weight(w):
    k, n = w.shape
    w = f64(np.asarray(w, np.float32).astype(ml_dtypes.bfloat16)).reshape(k // 32, 32, n)
    amax = np.abs(w).max(1)
    byte = np.clip(np.where(amax > 0, np.frexp(amax)[1] - 1 + 127 - 7, 1), 1, 254)
    scaled = (w * np.exp2(127.0 - byte)[:, None, :]).reshape(k, n).astype(np.float32)
    words = np.ascontiguousarray(scaled.reshape(k // 512, 128, 4, n).transpose(0, 1, 3, 2)).astype(ml_dtypes.float8_e4m3fn).view(np.uint8)
    return words, np.ascontiguousarray(byte.astype(np.uint8).reshape(k // 512, 16, n))


def unpack_weight(words, scales):
    g, p, n, _ = words.shape
    vals = np.ascontiguousarray(words).view(ml_dtypes.float8_e4m3fn).astype(np.float64) * np.repeat(np.exp2(scales.astype(np.float64) - 127.0), 8, axis=1)[..., None]
    return vals.transpose(0, 1, 3, 2).reshape(g * 512, n)

def planes(y):
    n, m = y.shape
    v = y.astype(np.float32).astype(ml_dtypes.bfloat16).astype(np.float64).reshape(n // 32, 32, m)
    top = np.abs(v).max(1)
    byte = np.clip(np.where(top > 0, np.frexp(top)[1] - 1 + 127 - 7, 1), 1, 254)
    codes = (v * np.exp2(127.0 - byte)[:, None, :]).reshape(n, m).astype(np.float32).astype(ml_dtypes.float8_e4m3fn).view(np.uint8)
    words = codes.reshape(n // 512, 128, 4, m).transpose(0, 1, 3, 2)
    return np.ascontiguousarray(words), np.ascontiguousarray(byte.astype(np.uint8).reshape(n // 512, 16, m))


K, T, S, N, G, H, J = 512, 2048, 512, 512, 2048, 512, 512


def setup_inputs():
    n = np.random.standard_normal
    s = mx_kscale(K)[:, None]
    u = mx_kscale(S)
    packed_xT = pack_weight(n((K, T)) * s)
    packed_dT = pack_weight(n((K, G)) / s)
    packed_w1 = pack_weight(n((H, N)) / np.sqrt(H) / u[:, None])
    return {
        "x_words": packed_xT[0],
        "x_scales": packed_xT[1],
        "d_words": packed_dT[0],
        "d_scales": packed_dT[1],
        "tab": np.random.uniform(0.4, 1.4, (H, J)).astype(np.float32),
        "gn": (np.random.uniform(0.5, 1.5, (H, 1)) * u[:, None]).astype(np.float32),
        "w1_words": packed_w1[0],
        "w1_scales": packed_w1[1],
        "offs": striped8(np.random.randint(0, T, (8, S))),
        "k1": striped8(np.random.randint(0, G, (8, H))),
        "n1": striped8(np.random.randint(0, J, (8, S))),
        "n2": striped8(np.stack([np.random.permutation(S) for _ in range(8)])),
        "n3": striped(np.random.randint(0, S, G)),
    }


def reference(x_words, x_scales, d_words, d_scales, tab, gn, w1_words, w1_scales, offs, k1, n1, n2, n3):
    d_k1 = unpack_weight(d_words, d_scales)[np.arange(K)[:, None], runs(k1, K)]
    xq = unpack_weight(x_words, x_scales)[np.arange(K)[:, None], runs(offs, K)]
    h = 0.0625 * (d_k1.T @ xq)
    z = f64(gn) * (h * (f64(tab)[np.arange(H)[:, None], runs(n1, H)]) - (0.5 * (h[np.arange(H)[:, None], runs(n2, H)])))
    h2 = unpack_weight(w1_words, w1_scales).T @ mxq(z, 0, "e4m3")
    mb = h2[:, unstriped(n3)]
    mx = mb.reshape(N, S, 4).max(axis=2)
    mn = mb.reshape(N, S, 4).min(axis=2)
    out_0 = mx * np.tanh(h2 - mn)
    return (out_0,) + planes(out_0)

@@ -1,0 +1,250 @@
+from contextlib import ExitStack
+
+import concourse.mybir as mybir
+
+F32 = mybir.dt.float32
+BF16 = mybir.dt.bfloat16
+I32 = mybir.dt.int32
+U32 = mybir.dt.uint32
+U16 = mybir.dt.uint16
+U8 = mybir.dt.uint8
+FP8X4 = mybir.dt.float8_e4m3fn_x4
+ALU = mybir.AluOpType
+ACT = mybir.ActivationFunctionType
+
+P = 128
+PACK = 4
+WIDTH = 512
+TABLE = 2048
+HALF = 256
+PER_COLUMN = 16
+MEMBERS = 4
+UNIT = 64
+RANGES = (256, 128, 64, 64)
+STEP = 256
+TAB_ON_SCALAR = (0,)
+
+FLOPS = 2 * 2 * WIDTH * WIDTH * WIDTH
+
+
+def entries(lists, first, count):
+    return lists[:, first // PER_COLUMN : (first + count) // PER_COLUMN]
+
+
+def deal(engine, out, in_, line):
+    engine.tensor_copy(
+        out=out.rearrange("p (t c i) -> p c t i", t=PACK, i=line),
+        in_=in_.rearrange("p (c i t) -> p c t i", t=PACK, i=line),
+    )
+
+
+def tile_picked_hpqkindggtan_none_po_kernel(
+    tc, x_words, x_scales, d_words, d_scales, tab, gn, w1_words, w1_scales, offs, k1, n1, n2, n3, out_0, out_1, out_2
+):
+    nc = tc.nc
+    with ExitStack() as ctx:
+        keep = ctx.enter_context(tc.tile_pool(name="keep", bufs=1))
+        shared = ctx.enter_context(tc.tile_pool(name="shared", bufs=1))
+        ring = ctx.enter_context(tc.tile_pool(name="ring", bufs=2))
+        psum = ctx.enter_context(tc.psum_pool(name="psum", bufs=1))
+
+        def held(name, shape, dtype):
+            return keep.tile(shape, dtype, name=name, align_bytes=64)
+
+        def as_words(packed):
+            return packed[0].rearrange("p n t -> p (n t)").bitcast(I32)
+
+        k1_sb = keep.tile([P, WIDTH // PER_COLUMN], U16, name="k1_sb")
+        offs_sb = keep.tile([P, WIDTH // PER_COLUMN], U16, name="offs_sb")
+        n1_sb = keep.tile([P, WIDTH // PER_COLUMN], U16, name="n1_sb")
+        n2_sb = keep.tile([P, WIDTH // PER_COLUMN], U16, name="n2_sb")
+        n3_sb = keep.tile([P, MEMBERS * WIDTH // PER_COLUMN], U16, name="n3_sb")
+        d_scale_table = held("d_scale_table", [P, TABLE], U8)
+        x_scale_table = held("x_scale_table", [P, TABLE], U8)
+        d_word_table = shared.tile([P, TABLE], U32, name="d_word_table", offset=0, align_bytes=64)
+        x_word_table = held("x_word_table", [P, TABLE], U32)
+        tab_sb = [held("tab_sb0", [P, WIDTH], F32)]
+        w1_scale_raw = held("w1_scale_raw", [P, WIDTH], U8)
+        gn_sb = held("gn_sb", [P, PACK], F32)
+        tab_rows = tab.rearrange("(p t) j -> p t j", t=PACK)
+
+        nc.vector.memset(d_scale_table[:].bitcast(I32), 0)
+        nc.vector.memset(x_scale_table[:].bitcast(I32), 0)
+        nc.vector.memset(w1_scale_raw[:].bitcast(I32), 0)
+        nc.sync.dma_start(k1_sb[:], k1)
+        nc.sync.dma_start(out=d_scale_table[0:P:8, :].bitcast(I32), in_=d_scales[0].bitcast(I32))
+        nc.sync.dma_start(offs_sb[:], offs)
+        nc.sync.dma_start(out=x_scale_table[0:P:8, :].bitcast(I32), in_=x_scales[0].bitcast(I32))
+        nc.sync.dma_start(out=w1_scale_raw[0:P:8, :].bitcast(I32), in_=w1_scales[0].bitcast(I32))
+        nc.sync.dma_start(out=d_word_table[:].bitcast(I32), in_=as_words(d_words))
+        nc.sync.dma_start(n1_sb[:], n1)
+        nc.sync.dma_start(n2_sb[:], n2)
+        nc.sync.dma_start(n3_sb[:], n3)
+        for t in TAB_ON_SCALAR:
+            nc.sync.dma_start(out=tab_sb[t][:], in_=tab_rows[:, t, :])
+        nc.sync.dma_start(out=x_word_table[:].bitcast(I32), in_=as_words(x_words))
+        nc.gpsimd.dma_start(out=gn_sb[:], in_=gn.rearrange("(p t) o -> p (t o)", t=PACK))
+        gain = held("gain", [P, PACK], F32)
+        nc.gpsimd.tensor_scalar(out=gain[:], in0=gn_sb[:], scalar1=0.0625, scalar2=0.0, op0=ALU.mult, op1=ALU.add)
+
+        d_scale_picked = held("d_scale_picked", [P, WIDTH], U8)
+        x_scale_picked = held("x_scale_picked", [P, WIDTH], U8)
+        scales = held("scales", [P, 3 * WIDTH], U8)
+        nc.vector.tensor_copy(d_scale_picked[:], d_scale_table[:].indirect(k1_sb[:]))
+        nc.vector.tensor_copy(x_scale_picked[:], x_scale_table[:].indirect(offs_sb[:]))
+        deal(nc.vector, scales[:, 0:WIDTH], d_scale_picked[:], 16)
+        nc.vector.tensor_copy(out=scales[:, WIDTH : 2 * WIDTH].bitcast(I32), in_=x_scale_picked[:].bitcast(I32))
+        deal(nc.vector, scales[:, 2 * WIDTH :], w1_scale_raw[:], 16)
+        for i in range(1, 4):
+            nc.scalar.dma_start(out=scales[i:P:32, :].bitcast(I32), in_=scales[8 * i : P : 32, :].bitcast(I32))
+
+        d_picked = held("d_picked", [P, WIDTH], U32)
+        d_dealt = held("d_dealt", [P, WIDTH], U32)
+        x_picked = [held("x_picked%d" % h, [P, HALF], U32) for h in range(2)]
+        nc.vector.tensor_copy(d_picked[:], d_word_table[:].indirect(k1_sb[:]))
+        deal(nc.vector, d_dealt[:].bitcast(I32), d_picked[:].bitcast(I32), 4)
+        w1_raw = shared.tile([P, WIDTH], U32, name="w1_raw", offset=0, align_bytes=64)
+        nc.sync.dma_start(out=w1_raw[:].bitcast(I32), in_=as_words(w1_words))
+        for t in range(1, PACK):
+            tab_sb.append(shared.tile([P, WIDTH], F32, name="tab_sb%d" % t, offset=4 * WIDTH * t, align_bytes=64))
+            nc.sync.dma_start(out=tab_sb[t][:], in_=tab_rows[:, t, :])
+        for h in range(2):
+            nc.vector.tensor_copy(x_picked[h][:], x_word_table[:].indirect(entries(offs_sb, h * HALF, HALF)))
+
+        kinds = {}
+        for t in TAB_ON_SCALAR:
+            kinds[t] = held("kinds%d" % t, [P, WIDTH], F32)
+            for h in range(2):
+                nc.scalar.activation(
+                    kinds[t][:, h * HALF : (h + 1) * HALF], tab_sb[t][:].indirect(entries(n1_sb, h * HALF, HALF)), ACT.Copy
+                )
+
+        h_banks = [psum.tile([P, WIDTH], F32, name="h_bank%d" % t, tag="bank%d" % t) for t in range(PACK)]
+        for t in range(PACK):
+            for h in range(2):
+                nc.tensor.matmul_mx(
+                    out=h_banks[t][:, h * HALF : (h + 1) * HALF],
+                    lhsT=d_dealt[:, t * P : (t + 1) * P].bitcast(FP8X4),
+                    lhsT_scale=scales[:, t * P : (t + 1) * P],
+                    rhs=x_picked[h][:].bitcast(FP8X4),
+                    rhs_scale=scales[:, WIDTH + h * HALF : WIDTH + (h + 1) * HALF],
+                    start=True,
+                    stop=True,
+                )
+
+        w1_dealt = held("w1_dealt", [P, WIDTH], U32)
+        deal(nc.vector, w1_dealt[:].bitcast(I32), w1_raw[:].bitcast(I32), 4)
+
+        gained = [held("gained%d" % t, [P, WIDTH], F32) for t in range(PACK)]
+        for t in range(PACK):
+            nc.scalar.activation(gained[t][:], h_banks[t][:], ACT.Copy, scale=gain[:, t : t + 1])
+
+        h2 = [held("h2_%d" % t, [P, WIDTH], F32) for t in range(PACK)]
+        for h in range(2):
+            cols = slice(h * HALF, (h + 1) * HALF)
+            product = held("product%d" % h, [P, PACK, HALF], F32)
+            partner = held("partner%d" % h, [P, PACK, HALF], F32)
+            for t in range(PACK):
+                if t in TAB_ON_SCALAR:
+                    kind = kinds[t][:, cols]
+                else:
+                    kind = tab_sb[t][:].indirect(entries(n1_sb, h * HALF, HALF))
+                nc.vector.tensor_tensor(product[:, t, :], kind, gained[t][:, cols], ALU.mult)
+                nc.scalar.activation(
+                    partner[:, t, :], gained[t][:].indirect(entries(n2_sb, h * HALF, HALF)), ACT.Copy, scale=-0.5
+                )
+            z = held("z%d" % h, [P, HALF, PACK], BF16)
+            nc.vector.tensor_tensor(
+                z[:].rearrange("p (c i) t -> p c t i", i=2),
+                product[:].rearrange("p t (c i) -> p c t i", i=2),
+                partner[:].rearrange("p t (c i) -> p c t i", i=2),
+                ALU.add,
+            )
+            z_words = held("z_words%d" % h, [P, HALF], U32)
+            z_scales = held("z_scales%d" % h, [P, HALF], U8)
+            nc.vector.quantize_mx(
+                out=z_words[:].bitcast(FP8X4), scales=z_scales[:], in_=z[:].rearrange("p j t -> p (j t)")
+            )
+            for t in range(PACK):
+                bank = psum.tile([P, HALF], F32, name="h2_bank%d_%d" % (h, t), tag="bank%d" % (t + PACK * (1 - h)))
+                nc.tensor.matmul_mx(
+                    out=bank[:],
+                    lhsT=w1_dealt[:, t * P : (t + 1) * P].bitcast(FP8X4),
+                    lhsT_scale=scales[:, 2 * WIDTH + t * P : 2 * WIDTH + (t + 1) * P],
+                    rhs=z_words[:].bitcast(FP8X4),
+                    rhs_scale=z_scales[:],
+                    start=True,
+                    stop=True,
+                )
+                if h == 1 and t > 0:
+                    nc.vector.tensor_copy(out=h2[t][:, cols], in_=bank[:])
+                else:
+                    nc.scalar.copy(out=h2[t][:, cols], in_=bank[:])
+
+        out_words = held("out_words", [P, WIDTH], U32)
+        out_scales = held("out_scales", [P, WIDTH], U8)
+        out_rows = out_0.rearrange("(p t) j -> p t j", t=PACK)
+        steps = []
+        first = 0
+        for width in RANGES:
+            result = held("result%d" % first, [P, PACK * width], F32)
+            tiles = STEP // width
+            for t0 in range(0, PACK, tiles):
+                steps.append((first, width, t0, tiles, result))
+            first = first + width
+
+        def extremes(number, first, width, t0, tiles):
+            members = ring.tile([P, MEMBERS * STEP], F32, name="members", align_bytes=64)
+            for u in range(STEP // UNIT):
+                t = t0 + u * UNIT // width
+                j = first + u * UNIT % width
+                picked = h2[t][:].indirect(entries(n3_sb, MEMBERS * j, MEMBERS * UNIT))
+                place = members[:, MEMBERS * u * UNIT : MEMBERS * (u + 1) * UNIT]
+                if number == 0 and u >= 2:
+                    nc.vector.tensor_copy(place, picked)
+                else:
+                    nc.scalar.activation(place, picked, ACT.Copy)
+            quads = members[:].rearrange("p (j e) -> p j e", e=MEMBERS)
+            larger = ring.tile([P, STEP, 2], F32, name="larger", align_bytes=64)
+            smaller = ring.tile([P, STEP, 2], F32, name="smaller", align_bytes=64)
+            nc.vector.tensor_tensor(smaller[:], quads[:, :, 0:2], quads[:, :, 2:4], ALU.min)
+            nc.vector.tensor_tensor(larger[:], quads[:, :, 0:2], quads[:, :, 2:4], ALU.max)
+            smallest = ring.tile([P, STEP], F32, name="smallest", align_bytes=64)
+            largest = ring.tile([P, STEP], F32, name="largest", align_bytes=64, bufs=3)
+            nc.vector.tensor_tensor(smallest[:], smaller[:, :, 0], smaller[:, :, 1], ALU.min)
+            nc.vector.tensor_tensor(largest[:], larger[:, :, 0], larger[:, :, 1], ALU.max)
+            gap = members[:, 0:STEP]
+            for i in range(tiles):
+                part = slice(i * width, (i + 1) * width)
+                nc.vector.tensor_tensor(gap[:, part], h2[t0 + i][:, first : first + width], smallest[:, part], ALU.subtract)
+            bent = ring.tile([P, STEP], F32, name="bent", align_bytes=64, bufs=3)
+            nc.scalar.activation(bent[:], gap, ACT.Tanh)
+            return largest, bent
+
+        def finish(first, width, t0, tiles, result, largest, bent):
+            cols = slice(first, first + width)
+            part = result[:, t0 * width : (t0 + tiles) * width]
+            nc.vector.tensor_tensor(part, largest[:], bent[:], ALU.mult)
+            nc.sync.dma_start(out=out_rows[:, t0 : t0 + tiles, cols], in_=part.rearrange("p (t j) -> p t j", t=tiles))
+            if t0 + tiles < PACK:
+                return
+            rounded = held("rounded%d" % first, [P, width * PACK], BF16)
+            nc.vector.tensor_copy(
+                out=rounded[:].rearrange("p (c i t) -> p c t i", t=PACK, i=4),
+                in_=result[:].rearrange("p (t c i) -> p c t i", t=PACK, i=4),
+            )
+            nc.vector.quantize_mx(out=out_words[:, cols].bitcast(FP8X4), scales=out_scales[:, cols], in_=rounded[:])
+            nc.sync.dma_start(out=as_words(out_1)[:, cols], in_=out_words[:, cols].bitcast(I32))
+
+        waiting = None
+        for number, (first, width, t0, tiles, result) in enumerate(steps):
+            made = extremes(number, first, width, t0, tiles)
+            if waiting is not None:
+                finish(*waiting)
+            waiting = (first, width, t0, tiles, result) + made
+        finish(*waiting)
+        for q in range(4):
+            queue = nc.sync if q % 2 == 0 else nc.scalar
+            queue.dma_start(
+                out=out_2[0][4 * q : 4 * q + 4, :].bitcast(I32), in_=out_scales[32 * q : 32 * q + 4, :].bitcast(I32)
+            )

@@ -19,10 +19,10 @@ TABLE = 2048
 HALF = 256
 PER_COLUMN = 16
 MEMBERS = 4
-UNIT = 64
-RANGES = (256, 128, 64, 64)
+WINDOW = 544
+RANGES = (256, 128, 128)
 STEP = 256
-TAB_ON_SCALAR = (0,)
+TAB_ON_SCALAR = (0, 1)
 
 FLOPS = 2 * 2 * WIDTH * WIDTH * WIDTH
 
@@ -59,42 +59,42 @@ def tile_picked_hpqkindggtan_none_po_kernel(
         n1_sb = keep.tile([P, WIDTH // PER_COLUMN], U16, name="n1_sb")
         n2_sb = keep.tile([P, WIDTH // PER_COLUMN], U16, name="n2_sb")
         n3_sb = keep.tile([P, MEMBERS * WIDTH // PER_COLUMN], U16, name="n3_sb")
-        d_scale_table = held("d_scale_table", [P, TABLE], U8)
+        d_scale_table = shared.tile([P, TABLE], U8, name="d_scale_table", offset=4 * TABLE, align_bytes=64)
         x_scale_table = held("x_scale_table", [P, TABLE], U8)
         d_word_table = shared.tile([P, TABLE], U32, name="d_word_table", offset=0, align_bytes=64)
         x_word_table = held("x_word_table", [P, TABLE], U32)
-        tab_sb = [held("tab_sb0", [P, WIDTH], F32)]
-        w1_scale_raw = held("w1_scale_raw", [P, WIDTH], U8)
+        tab_sb = [held("tab_sb%d" % t, [P, WIDTH], F32) for t in TAB_ON_SCALAR]
         gn_sb = held("gn_sb", [P, PACK], F32)
         tab_rows = tab.rearrange("(p t) j -> p t j", t=PACK)
 
+        warm = held("warm", [P, 8], F32)
+        warm_out = held("warm_out", [P, 8], F32)
         nc.vector.memset(d_scale_table[:].bitcast(I32), 0)
         nc.vector.memset(x_scale_table[:].bitcast(I32), 0)
-        nc.vector.memset(w1_scale_raw[:].bitcast(I32), 0)
+        nc.vector.memset(warm[:], 0.0)
         nc.sync.dma_start(k1_sb[:], k1)
-        nc.sync.dma_start(out=d_scale_table[0:P:8, :].bitcast(I32), in_=d_scales[0].bitcast(I32))
+        nc.scalar.dma_start(out=d_scale_table[0:P:8, :].bitcast(I32), in_=d_scales[0].bitcast(I32))
         nc.sync.dma_start(offs_sb[:], offs)
-        nc.sync.dma_start(out=x_scale_table[0:P:8, :].bitcast(I32), in_=x_scales[0].bitcast(I32))
-        nc.sync.dma_start(out=w1_scale_raw[0:P:8, :].bitcast(I32), in_=w1_scales[0].bitcast(I32))
-        nc.sync.dma_start(out=d_word_table[:].bitcast(I32), in_=as_words(d_words))
+        nc.scalar.dma_start(out=x_scale_table[0:P:8, :].bitcast(I32), in_=x_scales[0].bitcast(I32))
+        nc.scalar.activation(warm_out[:], warm[:], ACT.Tanh)
         nc.sync.dma_start(n1_sb[:], n1)
+        nc.sync.dma_start(out=d_word_table[:].bitcast(I32), in_=as_words(d_words))
+        nc.sync.dma_start(out=tab_sb[0][:], in_=tab_rows[:, 0, :])
+        nc.sync.dma_start(out=x_word_table[:].bitcast(I32), in_=as_words(x_words))
+        nc.sync.dma_start(out=tab_sb[1][:], in_=tab_rows[:, 1, :])
         nc.sync.dma_start(n2_sb[:], n2)
         nc.sync.dma_start(n3_sb[:], n3)
-        for t in TAB_ON_SCALAR:
-            nc.sync.dma_start(out=tab_sb[t][:], in_=tab_rows[:, t, :])
-        nc.sync.dma_start(out=x_word_table[:].bitcast(I32), in_=as_words(x_words))
         nc.gpsimd.dma_start(out=gn_sb[:], in_=gn.rearrange("(p t) o -> p (t o)", t=PACK))
         gain = held("gain", [P, PACK], F32)
         nc.gpsimd.tensor_scalar(out=gain[:], in0=gn_sb[:], scalar1=0.0625, scalar2=0.0, op0=ALU.mult, op1=ALU.add)
 
         d_scale_picked = held("d_scale_picked", [P, WIDTH], U8)
         x_scale_picked = held("x_scale_picked", [P, WIDTH], U8)
-        scales = held("scales", [P, 3 * WIDTH], U8)
+        scales = held("scales", [P, 2 * WIDTH], U8)
         nc.vector.tensor_copy(d_scale_picked[:], d_scale_table[:].indirect(k1_sb[:]))
         nc.vector.tensor_copy(x_scale_picked[:], x_scale_table[:].indirect(offs_sb[:]))
         deal(nc.vector, scales[:, 0:WIDTH], d_scale_picked[:], 16)
         nc.vector.tensor_copy(out=scales[:, WIDTH : 2 * WIDTH].bitcast(I32), in_=x_scale_picked[:].bitcast(I32))
-        deal(nc.vector, scales[:, 2 * WIDTH :], w1_scale_raw[:], 16)
         for i in range(1, 4):
             nc.scalar.dma_start(out=scales[i:P:32, :].bitcast(I32), in_=scales[8 * i : P : 32, :].bitcast(I32))
 
@@ -105,11 +105,15 @@ def tile_picked_hpqkindggtan_none_po_kernel(
         deal(nc.vector, d_dealt[:].bitcast(I32), d_picked[:].bitcast(I32), 4)
         w1_raw = shared.tile([P, WIDTH], U32, name="w1_raw", offset=0, align_bytes=64)
         nc.sync.dma_start(out=w1_raw[:].bitcast(I32), in_=as_words(w1_words))
-        for t in range(1, PACK):
+        for t in range(len(TAB_ON_SCALAR), PACK):
             tab_sb.append(shared.tile([P, WIDTH], F32, name="tab_sb%d" % t, offset=4 * WIDTH * t, align_bytes=64))
             nc.sync.dma_start(out=tab_sb[t][:], in_=tab_rows[:, t, :])
         for h in range(2):
             nc.vector.tensor_copy(x_picked[h][:], x_word_table[:].indirect(entries(offs_sb, h * HALF, HALF)))
+
+        w1_scale_raw = shared.tile([P, WIDTH], U8, name="w1_scale_raw", offset=4 * TABLE, align_bytes=64)
+        nc.vector.memset(w1_scale_raw[:].bitcast(I32), 0)
+        nc.sync.dma_start(out=w1_scale_raw[0:P:8, :].bitcast(I32), in_=w1_scales[0].bitcast(I32))
 
         kinds = {}
         for t in TAB_ON_SCALAR:
@@ -133,26 +137,38 @@ def tile_picked_hpqkindggtan_none_po_kernel(
                 )
 
         w1_dealt = held("w1_dealt", [P, WIDTH], U32)
+        w1_scale_dealt = held("w1_scale_dealt", [P, WIDTH], U8)
+        deal(nc.vector, w1_scale_dealt[:], w1_scale_raw[:], 16)
+        for i in range(1, 4):
+            nc.sync.dma_start(
+                out=w1_scale_dealt[i:P:32, :].bitcast(I32), in_=w1_scale_dealt[8 * i : P : 32, :].bitcast(I32)
+            )
         deal(nc.vector, w1_dealt[:].bitcast(I32), w1_raw[:].bitcast(I32), 4)
 
         gained = [held("gained%d" % t, [P, WIDTH], F32) for t in range(PACK)]
         for t in range(PACK):
-            nc.scalar.activation(gained[t][:], h_banks[t][:], ACT.Copy, scale=gain[:, t : t + 1])
+            if t != 1:
+                nc.scalar.activation(gained[t][:], h_banks[t][:], ACT.Copy, scale=gain[:, t : t + 1])
+            else:
+                nc.vector.tensor_scalar_mul(gained[t][:], h_banks[t][:], gain[:, t : t + 1])
 
-        h2 = [held("h2_%d" % t, [P, WIDTH], F32) for t in range(PACK)]
+        h2 = [held("h2_%d" % t, [P, WINDOW], F32) for t in range(PACK)]
+        products = [held("product%d" % h, [P, PACK, HALF], F32) for h in range(2)]
+        partners = [held("partner%d" % h, [P, PACK, HALF], F32) for h in range(2)]
+        for h in range(2):
+            for t in range(PACK):
+                paired = gained[t][:].indirect(entries(n2_sb, h * HALF, HALF))
+                nc.scalar.activation(partners[h][:, t, :], paired, ACT.Copy, scale=-0.5)
         for h in range(2):
             cols = slice(h * HALF, (h + 1) * HALF)
-            product = held("product%d" % h, [P, PACK, HALF], F32)
-            partner = held("partner%d" % h, [P, PACK, HALF], F32)
+            product = products[h]
+            partner = partners[h]
             for t in range(PACK):
                 if t in TAB_ON_SCALAR:
                     kind = kinds[t][:, cols]
                 else:
                     kind = tab_sb[t][:].indirect(entries(n1_sb, h * HALF, HALF))
                 nc.vector.tensor_tensor(product[:, t, :], kind, gained[t][:, cols], ALU.mult)
-                nc.scalar.activation(
-                    partner[:, t, :], gained[t][:].indirect(entries(n2_sb, h * HALF, HALF)), ACT.Copy, scale=-0.5
-                )
             z = held("z%d" % h, [P, HALF, PACK], BF16)
             nc.vector.tensor_tensor(
                 z[:].rearrange("p (c i) t -> p c t i", i=2),
@@ -170,7 +186,7 @@ def tile_picked_hpqkindggtan_none_po_kernel(
                 nc.tensor.matmul_mx(
                     out=bank[:],
                     lhsT=w1_dealt[:, t * P : (t + 1) * P].bitcast(FP8X4),
-                    lhsT_scale=scales[:, 2 * WIDTH + t * P : 2 * WIDTH + (t + 1) * P],
+                    lhsT_scale=w1_scale_dealt[:, t * P : (t + 1) * P],
                     rhs=z_words[:].bitcast(FP8X4),
                     rhs_scale=z_scales[:],
                     start=True,
@@ -193,14 +209,18 @@ def tile_picked_hpqkindggtan_none_po_kernel(
                 steps.append((first, width, t0, tiles, result))
             first = first + width
 
+        staged = [held("staged%d" % i, [P, MEMBERS * STEP], F32) for i in range(2)]
+
         def extremes(number, first, width, t0, tiles):
-            members = ring.tile([P, MEMBERS * STEP], F32, name="members", align_bytes=64)
-            for u in range(STEP // UNIT):
-                t = t0 + u * UNIT // width
-                j = first + u * UNIT % width
-                picked = h2[t][:].indirect(entries(n3_sb, MEMBERS * j, MEMBERS * UNIT))
-                place = members[:, MEMBERS * u * UNIT : MEMBERS * (u + 1) * UNIT]
-                if number == 0 and u >= 2:
+            members = staged[number % len(staged)]
+            pieces = max(2, tiles)
+            count = MEMBERS * STEP // pieces
+            for u in range(pieces):
+                t = t0 + u * tiles // pieces
+                entry = MEMBERS * first + u * count % (MEMBERS * width)
+                picked = h2[t][:].indirect(entries(n3_sb, entry, count))
+                place = members[:, u * count : (u + 1) * count]
+                if (number, u) in ((0, 1),):
                     nc.vector.tensor_copy(place, picked)
                 else:
                     nc.scalar.activation(place, picked, ACT.Copy)
@@ -213,7 +233,7 @@ def tile_picked_hpqkindggtan_none_po_kernel(
             largest = ring.tile([P, STEP], F32, name="largest", align_bytes=64, bufs=3)
             nc.vector.tensor_tensor(smallest[:], smaller[:, :, 0], smaller[:, :, 1], ALU.min)
             nc.vector.tensor_tensor(largest[:], larger[:, :, 0], larger[:, :, 1], ALU.max)
-            gap = members[:, 0:STEP]
+            gap = members[:, (MEMBERS - 1) * STEP :]
             for i in range(tiles):
                 part = slice(i * width, (i + 1) * width)
                 nc.vector.tensor_tensor(gap[:, part], h2[t0 + i][:, first : first + width], smallest[:, part], ALU.subtract)
@@ -229,7 +249,8 @@ def tile_picked_hpqkindggtan_none_po_kernel(
             if t0 + tiles < PACK:
                 return
             rounded = held("rounded%d" % first, [P, width * PACK], BF16)
-            nc.vector.tensor_copy(
+            round_off = nc.vector.tensor_copy if first in (0, 384) else nc.scalar.copy
+            round_off(
                 out=rounded[:].rearrange("p (c i t) -> p c t i", t=PACK, i=4),
                 in_=result[:].rearrange("p (t c i) -> p c t i", t=PACK, i=4),
             )

@@ -59,7 +59,7 @@ def tile_picked_hpqkindggtan_none_po_kernel(
         n1_sb = keep.tile([P, WIDTH // PER_COLUMN], U16, name="n1_sb")
         n2_sb = keep.tile([P, WIDTH // PER_COLUMN], U16, name="n2_sb")
         n3_sb = keep.tile([P, MEMBERS * WIDTH // PER_COLUMN], U16, name="n3_sb")
-        d_scale_table = shared.tile([P, TABLE], U8, name="d_scale_table", offset=4 * TABLE, align_bytes=64)
+        d_scale_table = held("d_scale_table", [P, TABLE], U8)
         x_scale_table = held("x_scale_table", [P, TABLE], U8)
         d_word_table = shared.tile([P, TABLE], U32, name="d_word_table", offset=0, align_bytes=64)
         x_word_table = held("x_word_table", [P, TABLE], U32)
@@ -69,14 +69,14 @@ def tile_picked_hpqkindggtan_none_po_kernel(
 
         warm = held("warm", [P, 8], F32)
         warm_out = held("warm_out", [P, 8], F32)
+        nc.gpsimd.memset(warm[:], 0.0)
+        nc.scalar.activation(warm_out[:], warm[:], ACT.Tanh)
         nc.vector.memset(d_scale_table[:].bitcast(I32), 0)
         nc.vector.memset(x_scale_table[:].bitcast(I32), 0)
-        nc.vector.memset(warm[:], 0.0)
         nc.sync.dma_start(k1_sb[:], k1)
-        nc.scalar.dma_start(out=d_scale_table[0:P:8, :].bitcast(I32), in_=d_scales[0].bitcast(I32))
+        nc.sync.dma_start(out=d_scale_table[0:P:8, :].bitcast(I32), in_=d_scales[0].bitcast(I32))
         nc.sync.dma_start(offs_sb[:], offs)
-        nc.scalar.dma_start(out=x_scale_table[0:P:8, :].bitcast(I32), in_=x_scales[0].bitcast(I32))
-        nc.scalar.activation(warm_out[:], warm[:], ACT.Tanh)
+        nc.sync.dma_start(out=x_scale_table[0:P:8, :].bitcast(I32), in_=x_scales[0].bitcast(I32))
         nc.sync.dma_start(n1_sb[:], n1)
         nc.sync.dma_start(out=d_word_table[:].bitcast(I32), in_=as_words(d_words))
         nc.sync.dma_start(out=tab_sb[0][:], in_=tab_rows[:, 0, :])
@@ -99,8 +99,11 @@ def tile_picked_hpqkindggtan_none_po_kernel(
             nc.scalar.dma_start(out=scales[i:P:32, :].bitcast(I32), in_=scales[8 * i : P : 32, :].bitcast(I32))
 
         d_picked = held("d_picked", [P, WIDTH], U32)
-        d_dealt = held("d_dealt", [P, WIDTH], U32)
-        x_picked = [held("x_picked%d" % h, [P, HALF], U32) for h in range(2)]
+        d_dealt = shared.tile([P, WIDTH], U32, name="d_dealt", offset=4 * TABLE, align_bytes=64)
+        x_picked = [
+            shared.tile([P, HALF], U32, name="x_picked%d" % h, offset=5 * TABLE + 4 * HALF * h, align_bytes=64)
+            for h in range(2)
+        ]
         nc.vector.tensor_copy(d_picked[:], d_word_table[:].indirect(k1_sb[:]))
         deal(nc.vector, d_dealt[:].bitcast(I32), d_picked[:].bitcast(I32), 4)
         w1_raw = shared.tile([P, WIDTH], U32, name="w1_raw", offset=0, align_bytes=64)
@@ -111,7 +114,7 @@ def tile_picked_hpqkindggtan_none_po_kernel(
         for h in range(2):
             nc.vector.tensor_copy(x_picked[h][:], x_word_table[:].indirect(entries(offs_sb, h * HALF, HALF)))
 
-        w1_scale_raw = shared.tile([P, WIDTH], U8, name="w1_scale_raw", offset=4 * TABLE, align_bytes=64)
+        w1_scale_raw = shared.tile([P, WIDTH], U8, name="w1_scale_raw", offset=4 * WIDTH, align_bytes=64)
         nc.vector.memset(w1_scale_raw[:].bitcast(I32), 0)
         nc.sync.dma_start(out=w1_scale_raw[0:P:8, :].bitcast(I32), in_=w1_scales[0].bitcast(I32))
 
@@ -147,42 +150,49 @@ def tile_picked_hpqkindggtan_none_po_kernel(
 
         gained = [held("gained%d" % t, [P, WIDTH], F32) for t in range(PACK)]
         for t in range(PACK):
-            if t != 1:
+            if True:
                 nc.scalar.activation(gained[t][:], h_banks[t][:], ACT.Copy, scale=gain[:, t : t + 1])
             else:
                 nc.vector.tensor_scalar_mul(gained[t][:], h_banks[t][:], gain[:, t : t + 1])
 
         h2 = [held("h2_%d" % t, [P, WINDOW], F32) for t in range(PACK)]
-        products = [held("product%d" % h, [P, PACK, HALF], F32) for h in range(2)]
-        partners = [held("partner%d" % h, [P, PACK, HALF], F32) for h in range(2)]
-        for h in range(2):
+        z = held("z", [P, HALF * PACK], BF16)
+        spans = []
+        first = 0
+        for width in (256, 256):
+            spans.append((first, width))
+            first = first + width
+        products = [held("product%d" % first, [P, PACK, width], F32) for first, width in spans]
+        partners = [held("partner0", [P, PACK, HALF], F32)]
+        for first, width in spans[1:]:
+            place = 4 * TABLE + 4 * PACK * (first - HALF)
+            partners.append(shared.tile([P, PACK, width], F32, name="partner%d" % first, offset=place, align_bytes=64))
+        for h, (first, width) in enumerate(spans):
             for t in range(PACK):
-                paired = gained[t][:].indirect(entries(n2_sb, h * HALF, HALF))
-                nc.scalar.activation(partners[h][:, t, :], paired, ACT.Copy, scale=-0.5)
-        for h in range(2):
-            cols = slice(h * HALF, (h + 1) * HALF)
-            product = products[h]
-            partner = partners[h]
+                paired = gained[t][:].indirect(entries(n2_sb, first, width))
+                if (h, t) in ():
+                    nc.vector.tensor_scalar(partners[h][:, t, :], paired, -0.5, 0.0, ALU.mult, ALU.add)
+                else:
+                    nc.scalar.activation(partners[h][:, t, :], paired, ACT.Copy, scale=-0.5)
+        for h, (first, width) in enumerate(spans):
+            cols = slice(first, first + width)
             for t in range(PACK):
                 if t in TAB_ON_SCALAR:
                     kind = kinds[t][:, cols]
                 else:
-                    kind = tab_sb[t][:].indirect(entries(n1_sb, h * HALF, HALF))
-                nc.vector.tensor_tensor(product[:, t, :], kind, gained[t][:, cols], ALU.mult)
-            z = held("z%d" % h, [P, HALF, PACK], BF16)
+                    kind = tab_sb[t][:].indirect(entries(n1_sb, first, width))
+                nc.vector.tensor_tensor(products[h][:, t, :], kind, gained[t][:, cols], ALU.mult)
             nc.vector.tensor_tensor(
-                z[:].rearrange("p (c i) t -> p c t i", i=2),
-                product[:].rearrange("p t (c i) -> p c t i", i=2),
-                partner[:].rearrange("p t (c i) -> p c t i", i=2),
+                z[:, 0 : PACK * width].rearrange("p (c i t) -> p c t i", t=PACK, i=2),
+                products[h][:].rearrange("p t (c i) -> p c t i", i=2),
+                partners[h][:].rearrange("p t (c i) -> p c t i", i=2),
                 ALU.add,
             )
-            z_words = held("z_words%d" % h, [P, HALF], U32)
-            z_scales = held("z_scales%d" % h, [P, HALF], U8)
-            nc.vector.quantize_mx(
-                out=z_words[:].bitcast(FP8X4), scales=z_scales[:], in_=z[:].rearrange("p j t -> p (j t)")
-            )
+            z_words = held("z_words%d" % h, [P, width], U32)
+            z_scales = held("z_scales%d" % h, [P, width], U8)
+            nc.vector.quantize_mx(out=z_words[:].bitcast(FP8X4), scales=z_scales[:], in_=z[:, 0 : PACK * width])
             for t in range(PACK):
-                bank = psum.tile([P, HALF], F32, name="h2_bank%d_%d" % (h, t), tag="bank%d" % (t + PACK * (1 - h)))
+                bank = psum.tile([P, width], F32, name="h2_bank%d_%d" % (h, t), tag="bank%d" % (t + PACK * ((h + 1) % 2)))
                 nc.tensor.matmul_mx(
                     out=bank[:],
                     lhsT=w1_dealt[:, t * P : (t + 1) * P].bitcast(FP8X4),
@@ -192,7 +202,7 @@ def tile_picked_hpqkindggtan_none_po_kernel(
                     start=True,
                     stop=True,
                 )
-                if h == 1 and t > 0:
+                if h == len(spans) - 1 and t > 0:
                     nc.vector.tensor_copy(out=h2[t][:, cols], in_=bank[:])
                 else:
                     nc.scalar.copy(out=h2[t][:, cols], in_=bank[:])

@@ -19,8 +19,8 @@ TABLE = 2048
 HALF = 256
 PER_COLUMN = 16
 MEMBERS = 4
-WINDOW = 544
-RANGES = (256, 128, 128)
+WINDOW = 1056
+RANGES = (128, 256, 128)
 STEP = 256
 TAB_ON_SCALAR = (0, 1)
 
@@ -202,7 +202,7 @@ def tile_picked_hpqkindggtan_none_po_kernel(
                     start=True,
                     stop=True,
                 )
-                if h == len(spans) - 1 and t > 0:
+                if h == 1 and t > 0:
                     nc.vector.tensor_copy(out=h2[t][:, cols], in_=bank[:])
                 else:
                     nc.scalar.copy(out=h2[t][:, cols], in_=bank[:])
@@ -223,14 +223,14 @@ def tile_picked_hpqkindggtan_none_po_kernel(
 
         def extremes(number, first, width, t0, tiles):
             members = staged[number % len(staged)]
-            pieces = max(2, tiles)
+            pieces = tiles
             count = MEMBERS * STEP // pieces
             for u in range(pieces):
                 t = t0 + u * tiles // pieces
                 entry = MEMBERS * first + u * count % (MEMBERS * width)
                 picked = h2[t][:].indirect(entries(n3_sb, entry, count))
                 place = members[:, u * count : (u + 1) * count]
-                if (number, u) in ((0, 1),):
+                if (number, u) in ((1, 0),):
                     nc.vector.tensor_copy(place, picked)
                 else:
                     nc.scalar.activation(place, picked, ACT.Copy)
@@ -242,11 +242,11 @@ def tile_picked_hpqkindggtan_none_po_kernel(
             smallest = ring.tile([P, STEP], F32, name="smallest", align_bytes=64)
             largest = ring.tile([P, STEP], F32, name="largest", align_bytes=64, bufs=3)
             nc.vector.tensor_tensor(smallest[:], smaller[:, :, 0], smaller[:, :, 1], ALU.min)
-            nc.vector.tensor_tensor(largest[:], larger[:, :, 0], larger[:, :, 1], ALU.max)
-            gap = members[:, (MEMBERS - 1) * STEP :]
+            gap = ring.tile([P, STEP], F32, name="gap", align_bytes=64)
             for i in range(tiles):
                 part = slice(i * width, (i + 1) * width)
                 nc.vector.tensor_tensor(gap[:, part], h2[t0 + i][:, first : first + width], smallest[:, part], ALU.subtract)
+            nc.vector.tensor_tensor(largest[:], larger[:, :, 0], larger[:, :, 1], ALU.max)
             bent = ring.tile([P, STEP], F32, name="bent", align_bytes=64, bufs=3)
             nc.scalar.activation(bent[:], gap, ACT.Tanh)
             return largest, bent
@@ -259,7 +259,7 @@ def tile_picked_hpqkindggtan_none_po_kernel(
             if t0 + tiles < PACK:
                 return
             rounded = held("rounded%d" % first, [P, width * PACK], BF16)
-            round_off = nc.vector.tensor_copy if first in (0, 384) else nc.scalar.copy
+            round_off = nc.vector.tensor_copy if first != 128 else nc.scalar.copy
             round_off(
                 out=rounded[:].rearrange("p (c i t) -> p c t i", t=PACK, i=4),
                 in_=result[:].rearrange("p (t c i) -> p c t i", t=PACK, i=4),

from contextlib import ExitStack

import concourse.mybir as mybir

F32 = mybir.dt.float32
BF16 = mybir.dt.bfloat16
I32 = mybir.dt.int32
U32 = mybir.dt.uint32
U16 = mybir.dt.uint16
U8 = mybir.dt.uint8
FP8X4 = mybir.dt.float8_e4m3fn_x4
ALU = mybir.AluOpType
ACT = mybir.ActivationFunctionType

P = 128
PACK = 4
WIDTH = 512
TABLE = 2048
HALF = 256
PER_COLUMN = 16
MEMBERS = 4
WINDOW = 1056
RANGES = (128, 256, 128)
STEP = 256
TAB_ON_SCALAR = (0, 1)

FLOPS = 2 * 2 * WIDTH * WIDTH * WIDTH


def entries(lists, first, count):
    return lists[:, first // PER_COLUMN : (first + count) // PER_COLUMN]


def deal(engine, out, in_, line):
    engine.tensor_copy(
        out=out.rearrange("p (t c i) -> p c t i", t=PACK, i=line),
        in_=in_.rearrange("p (c i t) -> p c t i", t=PACK, i=line),
    )


def tile_picked_hpqkindggtan_none_po_kernel(
    tc, x_words, x_scales, d_words, d_scales, tab, gn, w1_words, w1_scales, offs, k1, n1, n2, n3, out_0, out_1, out_2
):
    nc = tc.nc
    with ExitStack() as ctx:
        keep = ctx.enter_context(tc.tile_pool(name="keep", bufs=1))
        shared = ctx.enter_context(tc.tile_pool(name="shared", bufs=1))
        ring = ctx.enter_context(tc.tile_pool(name="ring", bufs=2))
        psum = ctx.enter_context(tc.psum_pool(name="psum", bufs=1))

        def held(name, shape, dtype):
            return keep.tile(shape, dtype, name=name, align_bytes=64)

        def as_words(packed):
            return packed[0].rearrange("p n t -> p (n t)").bitcast(I32)

        k1_sb = keep.tile([P, WIDTH // PER_COLUMN], U16, name="k1_sb")
        offs_sb = keep.tile([P, WIDTH // PER_COLUMN], U16, name="offs_sb")
        n1_sb = keep.tile([P, WIDTH // PER_COLUMN], U16, name="n1_sb")
        n2_sb = keep.tile([P, WIDTH // PER_COLUMN], U16, name="n2_sb")
        n3_sb = keep.tile([P, MEMBERS * WIDTH // PER_COLUMN], U16, name="n3_sb")
        d_scale_table = held("d_scale_table", [P, TABLE], U8)
        x_scale_table = held("x_scale_table", [P, TABLE], U8)
        d_word_table = shared.tile([P, TABLE], U32, name="d_word_table", offset=0, align_bytes=64)
        x_word_table = held("x_word_table", [P, TABLE], U32)
        tab_sb = [held("tab_sb%d" % t, [P, WIDTH], F32) for t in TAB_ON_SCALAR]
        gn_sb = held("gn_sb", [P, PACK], F32)
        tab_rows = tab.rearrange("(p t) j -> p t j", t=PACK)

        warm = held("warm", [P, 8], F32)
        warm_out = held("warm_out", [P, 8], F32)
        nc.gpsimd.memset(warm[:], 0.0)
        nc.scalar.activation(warm_out[:], warm[:], ACT.Tanh)
        nc.vector.memset(d_scale_table[:].bitcast(I32), 0)
        nc.vector.memset(x_scale_table[:].bitcast(I32), 0)
        nc.sync.dma_start(k1_sb[:], k1)
        nc.sync.dma_start(out=d_scale_table[0:P:8, :].bitcast(I32), in_=d_scales[0].bitcast(I32))
        nc.sync.dma_start(offs_sb[:], offs)
        nc.sync.dma_start(out=x_scale_table[0:P:8, :].bitcast(I32), in_=x_scales[0].bitcast(I32))
        nc.sync.dma_start(n1_sb[:], n1)
        nc.sync.dma_start(out=d_word_table[:].bitcast(I32), in_=as_words(d_words))
        nc.sync.dma_start(out=tab_sb[0][:], in_=tab_rows[:, 0, :])
        nc.sync.dma_start(out=x_word_table[:].bitcast(I32), in_=as_words(x_words))
        nc.sync.dma_start(out=tab_sb[1][:], in_=tab_rows[:, 1, :])
        nc.sync.dma_start(n2_sb[:], n2)
        nc.sync.dma_start(n3_sb[:], n3)
        nc.gpsimd.dma_start(out=gn_sb[:], in_=gn.rearrange("(p t) o -> p (t o)", t=PACK))
        gain = held("gain", [P, PACK], F32)
        nc.gpsimd.tensor_scalar(out=gain[:], in0=gn_sb[:], scalar1=0.0625, scalar2=0.0, op0=ALU.mult, op1=ALU.add)

        d_scale_picked = held("d_scale_picked", [P, WIDTH], U8)
        x_scale_picked = held("x_scale_picked", [P, WIDTH], U8)
        scales = held("scales", [P, 2 * WIDTH], U8)
        nc.vector.tensor_copy(d_scale_picked[:], d_scale_table[:].indirect(k1_sb[:]))
        nc.vector.tensor_copy(x_scale_picked[:], x_scale_table[:].indirect(offs_sb[:]))
        deal(nc.vector, scales[:, 0:WIDTH], d_scale_picked[:], 16)
        nc.vector.tensor_copy(out=scales[:, WIDTH : 2 * WIDTH].bitcast(I32), in_=x_scale_picked[:].bitcast(I32))
        for i in range(1, 4):
            nc.scalar.dma_start(out=scales[i:P:32, :].bitcast(I32), in_=scales[8 * i : P : 32, :].bitcast(I32))

        d_picked = held("d_picked", [P, WIDTH], U32)
        d_dealt = shared.tile([P, WIDTH], U32, name="d_dealt", offset=4 * TABLE, align_bytes=64)
        x_picked = [
            shared.tile([P, HALF], U32, name="x_picked%d" % h, offset=5 * TABLE + 4 * HALF * h, align_bytes=64)
            for h in range(2)
        ]
        nc.vector.tensor_copy(d_picked[:], d_word_table[:].indirect(k1_sb[:]))
        deal(nc.vector, d_dealt[:].bitcast(I32), d_picked[:].bitcast(I32), 4)
        w1_raw = shared.tile([P, WIDTH], U32, name="w1_raw", offset=0, align_bytes=64)
        nc.sync.dma_start(out=w1_raw[:].bitcast(I32), in_=as_words(w1_words))
        for t in range(len(TAB_ON_SCALAR), PACK):
            tab_sb.append(shared.tile([P, WIDTH], F32, name="tab_sb%d" % t, offset=4 * WIDTH * t, align_bytes=64))
            nc.sync.dma_start(out=tab_sb[t][:], in_=tab_rows[:, t, :])
        for h in range(2):
            nc.vector.tensor_copy(x_picked[h][:], x_word_table[:].indirect(entries(offs_sb, h * HALF, HALF)))

        w1_scale_raw = shared.tile([P, WIDTH], U8, name="w1_scale_raw", offset=4 * WIDTH, align_bytes=64)
        nc.vector.memset(w1_scale_raw[:].bitcast(I32), 0)
        nc.sync.dma_start(out=w1_scale_raw[0:P:8, :].bitcast(I32), in_=w1_scales[0].bitcast(I32))

        kinds = {}
        for t in TAB_ON_SCALAR:
            kinds[t] = held("kinds%d" % t, [P, WIDTH], F32)
            for h in range(2):
                nc.scalar.activation(
                    kinds[t][:, h * HALF : (h + 1) * HALF], tab_sb[t][:].indirect(entries(n1_sb, h * HALF, HALF)), ACT.Copy
                )

        h_banks = [psum.tile([P, WIDTH], F32, name="h_bank%d" % t, tag="bank%d" % t) for t in range(PACK)]
        for t in range(PACK):
            for h in range(2):
                nc.tensor.matmul_mx(
                    out=h_banks[t][:, h * HALF : (h + 1) * HALF],
                    lhsT=d_dealt[:, t * P : (t + 1) * P].bitcast(FP8X4),
                    lhsT_scale=scales[:, t * P : (t + 1) * P],
                    rhs=x_picked[h][:].bitcast(FP8X4),
                    rhs_scale=scales[:, WIDTH + h * HALF : WIDTH + (h + 1) * HALF],
                    start=True,
                    stop=True,
                )

        w1_dealt = held("w1_dealt", [P, WIDTH], U32)
        w1_scale_dealt = held("w1_scale_dealt", [P, WIDTH], U8)
        deal(nc.vector, w1_scale_dealt[:], w1_scale_raw[:], 16)
        for i in range(1, 4):
            nc.sync.dma_start(
                out=w1_scale_dealt[i:P:32, :].bitcast(I32), in_=w1_scale_dealt[8 * i : P : 32, :].bitcast(I32)
            )
        deal(nc.vector, w1_dealt[:].bitcast(I32), w1_raw[:].bitcast(I32), 4)

        gained = [held("gained%d" % t, [P, WIDTH], F32) for t in range(PACK)]
        for t in range(PACK):
            if True:
                nc.scalar.activation(gained[t][:], h_banks[t][:], ACT.Copy, scale=gain[:, t : t + 1])
            else:
                nc.vector.tensor_scalar_mul(gained[t][:], h_banks[t][:], gain[:, t : t + 1])

        h2 = [held("h2_%d" % t, [P, WINDOW], F32) for t in range(PACK)]
        z = held("z", [P, HALF * PACK], BF16)
        spans = []
        first = 0
        for width in (256, 256):
            spans.append((first, width))
            first = first + width
        products = [held("product%d" % first, [P, PACK, width], F32) for first, width in spans]
        partners = [held("partner0", [P, PACK, HALF], F32)]
        for first, width in spans[1:]:
            place = 4 * TABLE + 4 * PACK * (first - HALF)
            partners.append(shared.tile([P, PACK, width], F32, name="partner%d" % first, offset=place, align_bytes=64))
        for h, (first, width) in enumerate(spans):
            for t in range(PACK):
                paired = gained[t][:].indirect(entries(n2_sb, first, width))
                if (h, t) in ():
                    nc.vector.tensor_scalar(partners[h][:, t, :], paired, -0.5, 0.0, ALU.mult, ALU.add)
                else:
                    nc.scalar.activation(partners[h][:, t, :], paired, ACT.Copy, scale=-0.5)
        for h, (first, width) in enumerate(spans):
            cols = slice(first, first + width)
            for t in range(PACK):
                if t in TAB_ON_SCALAR:
                    kind = kinds[t][:, cols]
                else:
                    kind = tab_sb[t][:].indirect(entries(n1_sb, first, width))
                nc.vector.tensor_tensor(products[h][:, t, :], kind, gained[t][:, cols], ALU.mult)
            nc.vector.tensor_tensor(
                z[:, 0 : PACK * width].rearrange("p (c i t) -> p c t i", t=PACK, i=2),
                products[h][:].rearrange("p t (c i) -> p c t i", i=2),
                partners[h][:].rearrange("p t (c i) -> p c t i", i=2),
                ALU.add,
            )
            z_words = held("z_words%d" % h, [P, width], U32)
            z_scales = held("z_scales%d" % h, [P, width], U8)
            nc.vector.quantize_mx(out=z_words[:].bitcast(FP8X4), scales=z_scales[:], in_=z[:, 0 : PACK * width])
            for t in range(PACK):
                bank = psum.tile([P, width], F32, name="h2_bank%d_%d" % (h, t), tag="bank%d" % (t + PACK * ((h + 1) % 2)))
                nc.tensor.matmul_mx(
                    out=bank[:],
                    lhsT=w1_dealt[:, t * P : (t + 1) * P].bitcast(FP8X4),
                    lhsT_scale=w1_scale_dealt[:, t * P : (t + 1) * P],
                    rhs=z_words[:].bitcast(FP8X4),
                    rhs_scale=z_scales[:],
                    start=True,
                    stop=True,
                )
                if h == 1 and t > 0:
                    nc.vector.tensor_copy(out=h2[t][:, cols], in_=bank[:])
                else:
                    nc.scalar.copy(out=h2[t][:, cols], in_=bank[:])

        out_words = held("out_words", [P, WIDTH], U32)
        out_scales = held("out_scales", [P, WIDTH], U8)
        out_rows = out_0.rearrange("(p t) j -> p t j", t=PACK)
        steps = []
        first = 0
        for width in RANGES:
            result = held("result%d" % first, [P, PACK * width], F32)
            tiles = STEP // width
            for t0 in range(0, PACK, tiles):
                steps.append((first, width, t0, tiles, result))
            first = first + width

        staged = [held("staged%d" % i, [P, MEMBERS * STEP], F32) for i in range(2)]

        def extremes(number, first, width, t0, tiles):
            members = staged[number % len(staged)]
            pieces = tiles
            count = MEMBERS * STEP // pieces
            for u in range(pieces):
                t = t0 + u * tiles // pieces
                entry = MEMBERS * first + u * count % (MEMBERS * width)
                picked = h2[t][:].indirect(entries(n3_sb, entry, count))
                place = members[:, u * count : (u + 1) * count]
                if (number, u) in ((1, 0),):
                    nc.vector.tensor_copy(place, picked)
                else:
                    nc.scalar.activation(place, picked, ACT.Copy)
            quads = members[:].rearrange("p (j e) -> p j e", e=MEMBERS)
            larger = ring.tile([P, STEP, 2], F32, name="larger", align_bytes=64)
            smaller = ring.tile([P, STEP, 2], F32, name="smaller", align_bytes=64)
            nc.vector.tensor_tensor(smaller[:], quads[:, :, 0:2], quads[:, :, 2:4], ALU.min)
            nc.vector.tensor_tensor(larger[:], quads[:, :, 0:2], quads[:, :, 2:4], ALU.max)
            smallest = ring.tile([P, STEP], F32, name="smallest", align_bytes=64)
            largest = ring.tile([P, STEP], F32, name="largest", align_bytes=64, bufs=3)
            nc.vector.tensor_tensor(smallest[:], smaller[:, :, 0], smaller[:, :, 1], ALU.min)
            gap = ring.tile([P, STEP], F32, name="gap", align_bytes=64)
            for i in range(tiles):
                part = slice(i * width, (i + 1) * width)
                nc.vector.tensor_tensor(gap[:, part], h2[t0 + i][:, first : first + width], smallest[:, part], ALU.subtract)
            nc.vector.tensor_tensor(largest[:], larger[:, :, 0], larger[:, :, 1], ALU.max)
            bent = ring.tile([P, STEP], F32, name="bent", align_bytes=64, bufs=3)
            nc.scalar.activation(bent[:], gap, ACT.Tanh)
            return largest, bent

        def finish(first, width, t0, tiles, result, largest, bent):
            cols = slice(first, first + width)
            part = result[:, t0 * width : (t0 + tiles) * width]
            nc.vector.tensor_tensor(part, largest[:], bent[:], ALU.mult)
            nc.sync.dma_start(out=out_rows[:, t0 : t0 + tiles, cols], in_=part.rearrange("p (t j) -> p t j", t=tiles))
            if t0 + tiles < PACK:
                return
            rounded = held("rounded%d" % first, [P, width * PACK], BF16)
            round_off = nc.vector.tensor_copy if first != 128 else nc.scalar.copy
            round_off(
                out=rounded[:].rearrange("p (c i t) -> p c t i", t=PACK, i=4),
                in_=result[:].rearrange("p (t c i) -> p c t i", t=PACK, i=4),
            )
            nc.vector.quantize_mx(out=out_words[:, cols].bitcast(FP8X4), scales=out_scales[:, cols], in_=rounded[:])
            nc.sync.dma_start(out=as_words(out_1)[:, cols], in_=out_words[:, cols].bitcast(I32))

        waiting = None
        for number, (first, width, t0, tiles, result) in enumerate(steps):
            made = extremes(number, first, width, t0, tiles)
            if waiting is not None:
                finish(*waiting)
            waiting = (first, width, t0, tiles, result) + made
        finish(*waiting)
        for q in range(4):
            queue = nc.sync if q % 2 == 0 else nc.scalar
            queue.dma_start(
                out=out_2[0][4 * q : 4 * q + 4, :].bitcast(I32), in_=out_scales[32 * q : 32 * q + 4, :].bitcast(I32)
            )
